import numpy as np
import ml_dtypes


def mxq(x, axis, fmt="e4m3"):
    dtype, down = {"e4m3": (ml_dtypes.float8_e4m3fn, 7), "e5m2": (ml_dtypes.float8_e5m2, 14)}[fmt]
    v = np.moveaxis(np.asarray(x, np.float32).astype(ml_dtypes.bfloat16).astype(np.float64), axis, -1)
    blocks = v.reshape(v.shape[:-1] + (-1, 32))
    amax = np.abs(blocks).max(-1, keepdims=True)
    byte = np.maximum(np.where(amax > 0, np.frexp(amax)[1] - 1 + 127, 0) - down, 1)
    scale = np.exp2(byte - 127.0)
    codes = (blocks / scale).astype(np.float32).astype(dtype).astype(np.float64)
    return np.moveaxis((codes * scale).reshape(v.shape), -1, axis)


WIDE = False


def mx_kscale(k):
    if not WIDE:
        return np.ones(k)
    levels = np.array([10, -10, 5, -5, 0])
    if k % 512:
        return np.exp2(np.random.permutation(np.resize(levels, k // 32))).repeat(32)
    a = np.empty((k // 512, 16))
    for p in range(k // 512):
        a[p, :8] = np.random.permutation(np.resize(levels, 8))
        for g in range(8):
            far = levels[np.abs(levels - a[p, g]) >= 10]
            a[p, g + 8] = far[np.random.randint(len(far))]
    return np.exp2(a.ravel()).repeat(32)


def f64(x):
    return np.asarray(x).astype(np.float64)


def striped(idx):
    return np.tile(np.asarray(idx).reshape(-1, 16).T, (8, 1)).astype(np.uint16)


def unstriped(offs):
    return offs[:16].T.reshape(-1).astype(np.int64)


E2M1 = np.array([0.0, 0.5, 1.0, 1.5, 2.0, 3.0, 4.0, 6.0, -0.0, -0.5, -1.0, -1.5, -2.0, -3.0, -4.0, -6.0])


def pack_weight(w, fmt):
    k, n = w.shape
    w = f64(np.asarray(w, np.float32).astype(ml_dtypes.bfloat16)).reshape(k // 32, 32, n)
    amax = np.abs(w).max(1)
    if fmt == "e4m3":
        byte = np.frexp(amax)[1] - 1 + 127 - 7
    else:
        mant, ex = np.frexp(amax / 6.0)
        byte = np.where(mant > 0.5, ex, ex - 1) + 127
    byte = np.clip(np.where(amax > 0, byte, 1), 1, 254)
    scaled = (w * np.exp2(127.0 - byte)[:, None, :]).reshape(k, n).astype(np.float32)
    by_word = np.ascontiguousarray(scaled.reshape(k // 512, 128, 4, n).transpose(0, 1, 3, 2))
    if fmt == "e4m3":
        words = by_word.astype(ml_dtypes.float8_e4m3fn).view(np.uint8)
    else:
        c = by_word.astype(ml_dtypes.float4_e2m1fn).view(np.uint8) & 0xF
        words = (c[..., 0::2] | (c[..., 1::2] << 4)).reshape(k // 512, 128, 2 * n)
    return np.ascontiguousarray(words), np.ascontiguousarray(byte.astype(np.uint8).reshape(k // 512, 16, n))


def unpack_weight(words, scales, fmt):
    g, _, n = scales.shape
    words = np.ascontiguousarray(words).reshape(g, 128, n, -1)
    if fmt == "e4m3":
        vals = words.view(ml_dtypes.float8_e4m3fn).astype(np.float64)
    else:
        nib = np.empty((g, 128, n, 4), np.uint8)
        nib[..., 0::2] = words & 0xF
        nib[..., 1::2] = words >> 4
        vals = E2M1[nib]
    vals = vals * np.repeat(np.exp2(scales.astype(np.float64) - 127.0), 8, axis=1)[..., None]
    return vals.transpose(0, 1, 3, 2).reshape(g * 512, n)


def sigmoid(v):
    return 1.0 / (1.0 + np.exp(-v))


D, E, T, I, Q, G = 512, 512, 2048, 512, 128, 64


def setup_inputs():
    n = np.random.standard_normal
    idx = np.random.permutation(T)[:I]
    fd = mx_kscale(D)
    fe = mx_kscale(E)
    keysp = pack_weight(n((D, T)) / fd[:, None], "e2m1")
    valsp = pack_weight(n((E, T)) / fe[:, None], "e2m1")
    return {
        "query": (n((D, Q)) * 0.6 / np.sqrt(D) * fd[:, None]).astype(np.float32),
        "keys_words": keysp[0],
        "keys_scales": keysp[1],
        "gout": (n((E, Q)) * 1 / np.sqrt(E) * fe[:, None]).astype(np.float32),
        "vals_words": valsp[0],
        "vals_scales": valsp[1],
        "size": (np.random.uniform(0.5, 2.0, (1, I))).astype(np.float32),
        "base": (0.5 * n((Q, T))).astype(np.float32),
        "gq1": (np.random.uniform(0.3, 1.5, (Q, 1))).astype(np.float32),
        "offs": striped(idx),
    }


def reference(query, keys_words, keys_scales, gout, vals_words, vals_scales, size, base, gq1, offs):
    idx = unstriped(offs)
    keysu = unpack_weight(keys_words, keys_scales, "e2m1")
    valsu = unpack_weight(vals_words, vals_scales, "e2m1")
    queryq = mxq(f64(query), 0, "e4m3")
    keysidxg = keysu[:, idx]
    a = queryq.T @ keysidxg
    s = a.reshape(Q, G, I // G).mean(axis=2)
    p = np.exp(s - np.max(s, axis=1, keepdims=True))
    z = np.sum(p, axis=1, keepdims=True)
    r = p / z
    rr = np.repeat(r, I // G, axis=1)
    goutq = mxq(f64(gout), 0, "e4m3")
    valsidxg = valsu[:, idx]
    c0 = goutq.T @ valsidxg
    drr = c0 * f64(size) * sigmoid(a)
    dr = drr.reshape(Q, G, I // G).sum(axis=2)
    dz = np.sum(dr * p / np.square(z) * (-1.0), axis=1, keepdims=True)
    dp = dr / z + dz
    ds = dp * p
    e1 = ds / 8.0
    r1 = np.repeat(e1, I // G, axis=1)
    da = c0 * f64(size) * rr * sigmoid(a) * (1.0 - sigmoid(a)) + r1
    hda = da * 64.0 * 2.0 * 64.0
    he1 = hda.reshape(Q, G, I // G).sum(axis=2)
    hds = he1 / 8.0
    hdp = hds * p
    hdz = np.sum(hdp, axis=1, keepdims=True)
    hdr = hdp / z + hdz * (-1.0) / np.square(z) * p
    r51 = np.repeat(hdr, I // G, axis=1)
    hrr = hda * (1.0 - sigmoid(a)) * sigmoid(a) * c0 * f64(size)
    hr = hrr.reshape(Q, G, I // G).sum(axis=2)
    hz = np.sum(hdp * dr / np.square(z) * (-1.0), axis=1, keepdims=True) + np.sum(hdz * (-1.0) * dr * p / np.square(np.square(z)) * (-1.0), axis=1, keepdims=True) * z * 2.0 + np.sum(hr * p / np.square(z) * (-1.0), axis=1, keepdims=True)
    hp = hds * dp + hdz * (-1.0) / np.square(z) * dr + hr / z + hz
    hs = hp * p
    e52 = hs / 8.0
    r52 = np.repeat(e52, I // G, axis=1)
    ha = hda * (1.0 - sigmoid(a)) * c0 * f64(size) * rr * sigmoid(a) * (1.0 - sigmoid(a)) + hda * c0 * f64(size) * rr * sigmoid(a) * (-1.0) * sigmoid(a) * (1.0 - sigmoid(a)) + r51 * c0 * f64(size) * sigmoid(a) * (1.0 - sigmoid(a)) + r52
    gs = ha * f64(gq1)
    gf = np.zeros((Q, T))
    gf[:, idx] = gs
    y = f64(base) + gf
    return y

@@ -1,0 +1,217 @@
+from contextlib import ExitStack
+
+import concourse.mybir as mybir
+from concourse.masks import make_identity
+
+D, T, I, Q, G = 512, 2048, 512, 128, 64
+SPAN = I // G
+P = 128
+PACK = 4
+HALF = I // 2
+HALF_G = G // 2
+FLOPS = 2 * 2 * Q * D * I
+
+F32 = mybir.dt.float32
+BF16 = mybir.dt.bfloat16
+I32 = mybir.dt.int32
+U32 = mybir.dt.uint32
+U16 = mybir.dt.uint16
+U8 = mybir.dt.uint8
+FP8X4 = mybir.dt.float8_e4m3fn_x4
+FP4X4 = mybir.dt.float4_e2m1fn_x4
+ALU = mybir.AluOpType
+ACT = mybir.ActivationFunctionType
+AX = mybir.AxisListType
+
+OUT_CHUNKS = (256, 512, 512, 512, 256)
+
+
+def tile_attend_gpspanread_kernel(tc, query, keys_words, keys_scales, gout, vals_words, vals_scales, size, base, gq1, offs, out):
+    nc = tc.nc
+    with ExitStack() as ctx:
+        sb = ctx.enter_context(tc.tile_pool(name="sb", bufs=1))
+        ps = ctx.enter_context(tc.psum_pool(name="ps", bufs=1))
+
+        def tile(name, cols, dtype=F32):
+            return sb.tile([P, cols], dtype, name=name, align_bytes=64)
+
+        def spans(ap):
+            return ap.rearrange("p (g j) -> p g j", j=SPAN)
+
+        def per_slot(ap, groups=G):
+            return ap.unsqueeze(2).to_broadcast([P, groups, SPAN])
+
+        offsets = sb.tile([P, I // 16], U16, name="offsets")
+        v_bytes = tile("v_bytes", T, U8)
+        k_bytes = tile("k_bytes", T, U8)
+        v_words = tile("v_words", T, U16)
+        k_words = tile("k_words", T, U16)
+        gout_raw = sb.tile([P, PACK, Q], F32, name="gout_raw")
+        query_raw = sb.tile([P, PACK, Q], F32, name="query_raw")
+        size_col = tile("size_col", I // P)
+        gq = tile("gq", 1)
+        window = tile("window", T)
+        ident = tile("ident", P)
+        warm = tile("warm", 1)
+        warm_out = tile("warm_out", 1)
+
+        nc.vector.memset(v_bytes[:].bitcast(I32), 0)
+        nc.vector.memset(k_bytes[:].bitcast(I32), 0)
+        nc.vector.memset(warm[:], 0.0)
+        nc.scalar.activation(out=warm_out[:], in_=warm[:], func=ACT.Exp)
+        nc.vector.memset(window[:], 0.0)
+        make_identity(nc, ident[:])
+
+        def load_scale_rows(dst, src):
+            for quad in range(4):
+                nc.sync.dma_start(out=dst[32 * quad : 32 * quad + 4, :].bitcast(I32), in_=src[0, 4 * quad : 4 * quad + 4, :].bitcast(I32))
+
+        nc.sync.dma_start(offsets[:], offs)
+        load_scale_rows(v_bytes, vals_scales)
+        nc.sync.dma_start(out=v_words[:].bitcast(I32), in_=vals_words[0].bitcast(I32))
+        nc.sync.dma_start(out=gout_raw[:], in_=gout.rearrange("(p j) q -> p j q", j=PACK))
+        nc.sync.dma_start(out=k_words[:].bitcast(I32), in_=keys_words[0].bitcast(I32))
+        load_scale_rows(k_bytes, keys_scales)
+        nc.sync.dma_start(out=query_raw[:], in_=query.rearrange("(p j) q -> p j q", j=PACK))
+        with nc.allow_non_contiguous_dma(reason="one weight a slot, slots on the partitions"):
+            nc.sync.dma_start(out=size_col[:], in_=size.rearrange("o (b p) -> p (o b)", p=P))
+        nc.sync.dma_start(out=gq[:], in_=gq1)
+        base_tiles = []
+        first = 0
+        for n, width in enumerate(OUT_CHUNKS):
+            chunk = tile("base%d" % n, width)
+            nc.sync.dma_start(out=chunk[:], in_=base[:, first : first + width])
+            base_tiles.append((first, width, chunk))
+            first = first + width
+
+        def interleave(name, raw):
+            grouped = sb.tile([P, Q, PACK], BF16, name=name, align_bytes=64)
+            nc.scalar.copy(out=grouped[:], in_=raw[:].rearrange("p j q -> p q j"))
+            return grouped
+
+        def quantize(name, grouped):
+            codes = tile(name + "_codes", Q, U32)
+            scales = tile(name + "_scales", Q, U8)
+            nc.vector.quantize_mx(out=codes[:].bitcast(FP8X4), scales=scales[:], in_=grouped[:].rearrange("p q j -> p (q j)"))
+            return codes, scales
+
+        gout_bf = interleave("gout_bf", gout_raw)
+        query_bf = interleave("query_bf", query_raw)
+        vg_bytes = tile("vg_bytes", I, U8)
+        vg_words = tile("vg_words", I, U16)
+        nc.vector.tensor_copy(vg_bytes[:], v_bytes[:].indirect(offsets[:]))
+        nc.vector.tensor_copy(vg_words[:], v_words[:].indirect(offsets[:]))
+        gout_codes, gout_scales = quantize("gout", gout_bf)
+
+        c0_t = ps.tile([P, I], F32, name="c0_t")
+        u_t = tile("u_t", I)
+        u_banks = [ps.tile([P, I], F32, name="u%d" % h) for h in range(2)]
+        for b in range(I // P):
+            cols = slice(b * P, (b + 1) * P)
+            nc.tensor.matmul_mx(out=c0_t[:, cols], lhsT=vg_words[:, cols].bitcast(FP4X4), lhsT_scale=vg_bytes[:, cols],
+                                rhs=gout_codes[:].bitcast(FP8X4), rhs_scale=gout_scales[:], start=True, stop=True)
+        for b in range(I // P):
+            cols = slice(b * P, (b + 1) * P)
+            nc.scalar.activation(out=u_t[:, cols], in_=c0_t[:, cols], func=ACT.Copy, scale=size_col[:, b : b + 1])
+        for b in range(I // P):
+            cols = slice(b * P, (b + 1) * P)
+            nc.tensor.transpose(u_banks[b // 2][:, (b % 2) * P : (b % 2 + 1) * P], u_t[:, cols], ident[:])
+
+        cq = tile("cq", 1)
+        nc.scalar.activation(out=cq[:], in_=gq[:], func=ACT.Copy, scale=128.0)
+        a_banks = [ps.tile([P, I], F32, name="a%d" % h) for h in range(2)]
+        query_codes, query_scales = quantize("query", query_bf)
+        for h in range(2):
+            kg_words = tile("kg_words%d" % h, HALF, U16)
+            kg_bytes = tile("kg_bytes%d" % h, HALF, U8)
+            part = offsets[:, h * HALF // 16 : (h + 1) * HALF // 16]
+            nc.vector.tensor_copy(kg_words[:], k_words[:].indirect(part))
+            nc.vector.tensor_copy(kg_bytes[:], k_bytes[:].indirect(part))
+            nc.tensor.matmul_mx(out=a_banks[h][:, 0:HALF], lhsT=query_codes[:].bitcast(FP8X4), lhsT_scale=query_scales[:],
+                                rhs=kg_words[:].bitcast(FP4X4), rhs_scale=kg_bytes[:], start=True, stop=True)
+
+        t = tile("t", I)
+        e = tile("e", I)
+        w = tile("w", I)
+        w_sq = tile("w_sq", I)
+        s_sum = tile("s_sum", G)
+        neg_s = tile("neg_s", G)
+        neg_max = tile("neg_max", 1)
+        p = tile("p", G)
+        z = tile("z", 1)
+        rz = tile("rz", 1)
+        r = tile("r", G)
+        r2 = tile("r2", G)
+
+        def half(h):
+            return slice(h * HALF, (h + 1) * HALF)
+
+        def tanh_and_sum(h):
+            nc.scalar.activation(out=t[:, half(h)], in_=a_banks[h][:, 0:HALF], func=ACT.Tanh, scale=0.5)
+            nc.vector.tensor_reduce(out=s_sum[:, h * HALF_G : (h + 1) * HALF_G], in_=spans(a_banks[h][:, 0:HALF]), axis=AX.X, op=ALU.add)
+
+        def e_and_w(h):
+            nc.vector.scalar_tensor_tensor(out=e[:, half(h)], in0=t[:, half(h)], scalar=1.0, in1=u_banks[h][:, 0:HALF], op0=ALU.add, op1=ALU.mult)
+            nc.vector.scalar_tensor_tensor(out=w[:, half(h)], in0=t[:, half(h)], scalar=1.0, in1=e[:, half(h)], op0=ALU.subtract, op1=ALU.mult)
+
+        tanh_and_sum(0)
+        e_and_w(0)
+        tanh_and_sum(1)
+        nc.vector.tensor_scalar(out=neg_s[:], in0=s_sum[:], scalar1=-1.0 / SPAN, scalar2=None, op0=ALU.mult, op1=ALU.min, accum_out=neg_max[:])
+        nc.scalar.activation(out=w_sq[:, half(0)], in_=w[:, half(0)], func=ACT.Square)
+        nc.scalar.activation(out=p[:], in_=neg_s[:], func=ACT.Exp, scale=-1.0, bias=neg_max[:], accum_out=z[:])
+        e_and_w(1)
+        nc.vector.reciprocal(out=rz[:], in_=z[:])
+        nc.scalar.activation(out=w_sq[:, half(1)], in_=w[:, half(1)], func=ACT.Square)
+        nc.scalar.activation(out=r[:], in_=p[:], func=ACT.Copy, scale=rz[:])
+        nc.scalar.activation(out=r2[:], in_=p[:], func=ACT.Square, scale=rz[:])
+
+        ge = sb.tile([P, 2, G], F32, name="ge")
+        e_sum = ge[:, 1, :]
+        g2 = ge[:, 0, :]
+        w_sum = tile("w_sum", G)
+        wsq_sum = tile("wsq_sum", G)
+        nc.vector.tensor_reduce(out=e_sum, in_=spans(e[:]), axis=AX.X, op=ALU.add)
+        nc.vector.tensor_reduce(out=w_sum[:], in_=spans(w[:]), axis=AX.X, op=ALU.add)
+
+        re = tile("re", G)
+        d = tile("d", 1)
+        g1 = tile("g1", G)
+        rh = tile("rh", G)
+        hh = tile("hh", 1)
+        kr = sb.tile([P, 2, G], F32, name="kr")
+        gam = tile("gam", G)
+        yr = tile("yr", G)
+        zz = tile("zz", G)
+        qq = tile("qq", G)
+        qbar = tile("qbar", 1)
+        delta = tile("delta", G)
+        delta_slot = tile("delta_slot", I)
+        tg = tile("tg", I)
+        n0 = tile("n0", I)
+        m = tile("m", I)
+        k = tile("k", I)
+        f = tile("f", I)
+
+        nc.vector.scalar_tensor_tensor(out=re[:], in0=e_sum, scalar=1.0, in1=r[:], op0=ALU.mult, op1=ALU.mult, accum_out=d[:])
+        nc.vector.scalar_tensor_tensor(out=g1[:], in0=w_sum[:], scalar=-0.5, in1=e_sum, op0=ALU.mult, op1=ALU.add)
+        nc.vector.tensor_tensor(out=g2, in0=e_sum, in1=w_sum[:], op=ALU.subtract)
+        nc.vector.tensor_reduce(out=wsq_sum[:], in_=spans(w_sq[:]), axis=AX.X, op=ALU.add)
+        nc.vector.scalar_tensor_tensor(out=rh[:], in0=g1[:], scalar=d[:], in1=r2[:], op0=ALU.subtract, op1=ALU.mult, accum_out=hh[:])
+        nc.vector.scalar_tensor_tensor(out=kr[:], in0=ge[:], scalar=d[:], in1=r[:].unsqueeze(1).to_broadcast([P, 2, G]), op0=ALU.subtract, op1=ALU.mult)
+        nc.vector.scalar_tensor_tensor(out=spans(tg[:]), in0=spans(t[:]), scalar=cq[:], in1=per_slot(r2[:]), op0=ALU.mult, op1=ALU.mult)
+        nc.vector.scalar_tensor_tensor(out=yr[:], in0=kr[:, 0, :], scalar=hh[:], in1=kr[:, 1, :], op0=ALU.subtract, op1=ALU.mult)
+        nc.vector.scalar_tensor_tensor(out=zz[:], in0=wsq_sum[:], scalar=-0.5, in1=r2[:], op0=ALU.mult, op1=ALU.mult)
+        nc.vector.scalar_tensor_tensor(out=gam[:], in0=r[:], scalar=hh[:], in1=rh[:], op0=ALU.mult, op1=ALU.subtract)
+        nc.vector.scalar_tensor_tensor(out=spans(n0[:]), in0=spans(w[:]), scalar=-4.0, in1=per_slot(e_sum), op0=ALU.mult, op1=ALU.add)
+        nc.vector.scalar_tensor_tensor(out=qq[:], in0=yr[:], scalar=-0.25, in1=zz[:], op0=ALU.mult, op1=ALU.add, accum_out=qbar[:])
+        nc.vector.scalar_tensor_tensor(out=m[:], in0=n0[:], scalar=d[:], in1=tg[:], op0=ALU.subtract, op1=ALU.mult)
+        nc.vector.scalar_tensor_tensor(out=delta[:], in0=r[:], scalar=qbar[:], in1=qq[:], op0=ALU.mult, op1=ALU.subtract)
+        nc.scalar.activation(out=spans(delta_slot[:]), in_=per_slot(delta[:]), func=ACT.Copy, scale=cq[:])
+        nc.vector.scalar_tensor_tensor(out=spans(k[:]), in0=per_slot(gam[:]), scalar=cq[:], in1=spans(m[:]), op0=ALU.mult, op1=ALU.add)
+        nc.vector.tensor_tensor(out=f[:], in0=k[:], in1=w[:], op=ALU.mult)
+        nc.vector.tensor_tensor(out=window[:].indirect(offsets[:]), in0=f[:], in1=delta_slot[:], op=ALU.add)
+
+        for first, width, chunk in base_tiles:
+            nc.vector.tensor_tensor(out=chunk[:], in0=window[:, first : first + width], in1=chunk[:], op=ALU.add)
+            nc.sync.dma_start(out=out[:, first : first + width], in_=chunk[:])

@@ -23,7 +23,7 @@ ALU = mybir.AluOpType
 ACT = mybir.ActivationFunctionType
 AX = mybir.AxisListType
 
-OUT_CHUNKS = (256, 512, 512, 512, 256)
+OUT_CHUNKS = (256, 384, 384, 384, 384, 256)
 
 
 def tile_attend_gpspanread_kernel(tc, query, keys_words, keys_scales, gout, vals_words, vals_scales, size, base, gq1, offs, out):
@@ -33,7 +33,7 @@ def tile_attend_gpspanread_kernel(tc, query, keys_words, keys_scales, gout, vals
         ps = ctx.enter_context(tc.psum_pool(name="ps", bufs=1))
 
         def tile(name, cols, dtype=F32):
-            return sb.tile([P, cols], dtype, name=name, align_bytes=64)
+            return sb.tile([P, cols], dtype, name=name, tag=name, align_bytes=64)
 
         def spans(ap):
             return ap.rearrange("p (g j) -> p g j", j=SPAN)
@@ -56,10 +56,10 @@ def tile_attend_gpspanread_kernel(tc, query, keys_words, keys_scales, gout, vals
         warm_out = tile("warm_out", 1)
 
         nc.vector.memset(v_bytes[:].bitcast(I32), 0)
-        nc.vector.memset(k_bytes[:].bitcast(I32), 0)
+        nc.gpsimd.memset(k_bytes[:].bitcast(I32), 0)
         nc.vector.memset(warm[:], 0.0)
         nc.scalar.activation(out=warm_out[:], in_=warm[:], func=ACT.Exp)
-        nc.vector.memset(window[:], 0.0)
+        nc.vector.memset(window[:].bitcast(I32), 0)
         make_identity(nc, ident[:])
 
         def load_scale_rows(dst, src):
@@ -67,22 +67,15 @@ def tile_attend_gpspanread_kernel(tc, query, keys_words, keys_scales, gout, vals
                 nc.sync.dma_start(out=dst[32 * quad : 32 * quad + 4, :].bitcast(I32), in_=src[0, 4 * quad : 4 * quad + 4, :].bitcast(I32))
 
         nc.sync.dma_start(offsets[:], offs)
-        load_scale_rows(v_bytes, vals_scales)
         nc.sync.dma_start(out=v_words[:].bitcast(I32), in_=vals_words[0].bitcast(I32))
+        load_scale_rows(v_bytes, vals_scales)
         nc.sync.dma_start(out=gout_raw[:], in_=gout.rearrange("(p j) q -> p j q", j=PACK))
         nc.sync.dma_start(out=k_words[:].bitcast(I32), in_=keys_words[0].bitcast(I32))
-        load_scale_rows(k_bytes, keys_scales)
-        nc.sync.dma_start(out=query_raw[:], in_=query.rearrange("(p j) q -> p j q", j=PACK))
         with nc.allow_non_contiguous_dma(reason="one weight a slot, slots on the partitions"):
             nc.sync.dma_start(out=size_col[:], in_=size.rearrange("o (b p) -> p (o b)", p=P))
+        nc.sync.dma_start(out=query_raw[:], in_=query.rearrange("(p j) q -> p j q", j=PACK))
+        load_scale_rows(k_bytes, keys_scales)
         nc.sync.dma_start(out=gq[:], in_=gq1)
-        base_tiles = []
-        first = 0
-        for n, width in enumerate(OUT_CHUNKS):
-            chunk = tile("base%d" % n, width)
-            nc.sync.dma_start(out=chunk[:], in_=base[:, first : first + width])
-            base_tiles.append((first, width, chunk))
-            first = first + width
 
         def interleave(name, raw):
             grouped = sb.tile([P, Q, PACK], BF16, name=name, align_bytes=64)
@@ -99,8 +92,8 @@ def tile_attend_gpspanread_kernel(tc, query, keys_words, keys_scales, gout, vals
         query_bf = interleave("query_bf", query_raw)
         vg_bytes = tile("vg_bytes", I, U8)
         vg_words = tile("vg_words", I, U16)
-        nc.vector.tensor_copy(vg_bytes[:], v_bytes[:].indirect(offsets[:]))
         nc.vector.tensor_copy(vg_words[:], v_words[:].indirect(offsets[:]))
+        nc.vector.tensor_copy(vg_bytes[:], v_bytes[:].indirect(offsets[:]))
         gout_codes, gout_scales = quantize("gout", gout_bf)
 
         c0_t = ps.tile([P, I], F32, name="c0_t")
@@ -117,18 +110,25 @@ def tile_attend_gpspanread_kernel(tc, query, keys_words, keys_scales, gout, vals
             cols = slice(b * P, (b + 1) * P)
             nc.tensor.transpose(u_banks[b // 2][:, (b % 2) * P : (b % 2 + 1) * P], u_t[:, cols], ident[:])
 
-        cq = tile("cq", 1)
-        nc.scalar.activation(out=cq[:], in_=gq[:], func=ACT.Copy, scale=128.0)
         a_banks = [ps.tile([P, I], F32, name="a%d" % h) for h in range(2)]
+
+        def list_half(h):
+            return offsets[:, h * HALF // 16 : (h + 1) * HALF // 16]
+
+        kg_words = tile("kg_words", I, U16)
+        nc.vector.tensor_copy(kg_words[:], k_words[:].indirect(offsets[:]))
         query_codes, query_scales = quantize("query", query_bf)
         for h in range(2):
-            kg_words = tile("kg_words%d" % h, HALF, U16)
             kg_bytes = tile("kg_bytes%d" % h, HALF, U8)
-            part = offsets[:, h * HALF // 16 : (h + 1) * HALF // 16]
-            nc.vector.tensor_copy(kg_words[:], k_words[:].indirect(part))
-            nc.vector.tensor_copy(kg_bytes[:], k_bytes[:].indirect(part))
+            nc.vector.tensor_copy(kg_bytes[:], k_bytes[:].indirect(list_half(h)))
             nc.tensor.matmul_mx(out=a_banks[h][:, 0:HALF], lhsT=query_codes[:].bitcast(FP8X4), lhsT_scale=query_scales[:],
-                                rhs=kg_words[:].bitcast(FP4X4), rhs_scale=kg_bytes[:], start=True, stop=True)
+                                rhs=kg_words[:, h * HALF : (h + 1) * HALF].bitcast(FP4X4), rhs_scale=kg_bytes[:], start=True, stop=True)
+
+        base_halves = []
+        for h, tag in enumerate(("v_words", "k_words")):
+            base_half = sb.tile([P, T // 2], F32, name="base%d" % h, tag=tag, align_bytes=64)
+            nc.sync.dma_start(out=base_half[:], in_=base[:, h * T // 2 : (h + 1) * T // 2])
+            base_halves.append(base_half)
 
         t = tile("t", I)
         e = tile("e", I)
@@ -143,37 +143,11 @@ def tile_attend_gpspanread_kernel(tc, query, keys_words, keys_scales, gout, vals
         r = tile("r", G)
         r2 = tile("r2", G)
 
-        def half(h):
-            return slice(h * HALF, (h + 1) * HALF)
-
-        def tanh_and_sum(h):
-            nc.scalar.activation(out=t[:, half(h)], in_=a_banks[h][:, 0:HALF], func=ACT.Tanh, scale=0.5)
-            nc.vector.tensor_reduce(out=s_sum[:, h * HALF_G : (h + 1) * HALF_G], in_=spans(a_banks[h][:, 0:HALF]), axis=AX.X, op=ALU.add)
-
-        def e_and_w(h):
-            nc.vector.scalar_tensor_tensor(out=e[:, half(h)], in0=t[:, half(h)], scalar=1.0, in1=u_banks[h][:, 0:HALF], op0=ALU.add, op1=ALU.mult)
-            nc.vector.scalar_tensor_tensor(out=w[:, half(h)], in0=t[:, half(h)], scalar=1.0, in1=e[:, half(h)], op0=ALU.subtract, op1=ALU.mult)
-
-        tanh_and_sum(0)
-        e_and_w(0)
-        tanh_and_sum(1)
-        nc.vector.tensor_scalar(out=neg_s[:], in0=s_sum[:], scalar1=-1.0 / SPAN, scalar2=None, op0=ALU.mult, op1=ALU.min, accum_out=neg_max[:])
-        nc.scalar.activation(out=w_sq[:, half(0)], in_=w[:, half(0)], func=ACT.Square)
-        nc.scalar.activation(out=p[:], in_=neg_s[:], func=ACT.Exp, scale=-1.0, bias=neg_max[:], accum_out=z[:])
-        e_and_w(1)
-        nc.vector.reciprocal(out=rz[:], in_=z[:])
-        nc.scalar.activation(out=w_sq[:, half(1)], in_=w[:, half(1)], func=ACT.Square)
-        nc.scalar.activation(out=r[:], in_=p[:], func=ACT.Copy, scale=rz[:])
-        nc.scalar.activation(out=r2[:], in_=p[:], func=ACT.Square, scale=rz[:])
-
         ge = sb.tile([P, 2, G], F32, name="ge")
         e_sum = ge[:, 1, :]
         g2 = ge[:, 0, :]
         w_sum = tile("w_sum", G)
         wsq_sum = tile("wsq_sum", G)
-        nc.vector.tensor_reduce(out=e_sum, in_=spans(e[:]), axis=AX.X, op=ALU.add)
-        nc.vector.tensor_reduce(out=w_sum[:], in_=spans(w[:]), axis=AX.X, op=ALU.add)
-
         re = tile("re", G)
         d = tile("d", 1)
         g1 = tile("g1", G)
@@ -193,25 +167,87 @@ def tile_attend_gpspanread_kernel(tc, query, keys_words, keys_scales, gout, vals
         k = tile("k", I)
         f = tile("f", I)
 
-        nc.vector.scalar_tensor_tensor(out=re[:], in0=e_sum, scalar=1.0, in1=r[:], op0=ALU.mult, op1=ALU.mult, accum_out=d[:])
-        nc.vector.scalar_tensor_tensor(out=g1[:], in0=w_sum[:], scalar=-0.5, in1=e_sum, op0=ALU.mult, op1=ALU.add)
-        nc.vector.tensor_tensor(out=g2, in0=e_sum, in1=w_sum[:], op=ALU.subtract)
-        nc.vector.tensor_reduce(out=wsq_sum[:], in_=spans(w_sq[:]), axis=AX.X, op=ALU.add)
-        nc.vector.scalar_tensor_tensor(out=rh[:], in0=g1[:], scalar=d[:], in1=r2[:], op0=ALU.subtract, op1=ALU.mult, accum_out=hh[:])
-        nc.vector.scalar_tensor_tensor(out=kr[:], in0=ge[:], scalar=d[:], in1=r[:].unsqueeze(1).to_broadcast([P, 2, G]), op0=ALU.subtract, op1=ALU.mult)
-        nc.vector.scalar_tensor_tensor(out=spans(tg[:]), in0=spans(t[:]), scalar=cq[:], in1=per_slot(r2[:]), op0=ALU.mult, op1=ALU.mult)
-        nc.vector.scalar_tensor_tensor(out=yr[:], in0=kr[:, 0, :], scalar=hh[:], in1=kr[:, 1, :], op0=ALU.subtract, op1=ALU.mult)
-        nc.vector.scalar_tensor_tensor(out=zz[:], in0=wsq_sum[:], scalar=-0.5, in1=r2[:], op0=ALU.mult, op1=ALU.mult)
-        nc.vector.scalar_tensor_tensor(out=gam[:], in0=r[:], scalar=hh[:], in1=rh[:], op0=ALU.mult, op1=ALU.subtract)
-        nc.vector.scalar_tensor_tensor(out=spans(n0[:]), in0=spans(w[:]), scalar=-4.0, in1=per_slot(e_sum), op0=ALU.mult, op1=ALU.add)
-        nc.vector.scalar_tensor_tensor(out=qq[:], in0=yr[:], scalar=-0.25, in1=zz[:], op0=ALU.mult, op1=ALU.add, accum_out=qbar[:])
-        nc.vector.scalar_tensor_tensor(out=m[:], in0=n0[:], scalar=d[:], in1=tg[:], op0=ALU.subtract, op1=ALU.mult)
-        nc.vector.scalar_tensor_tensor(out=delta[:], in0=r[:], scalar=qbar[:], in1=qq[:], op0=ALU.mult, op1=ALU.subtract)
-        nc.scalar.activation(out=spans(delta_slot[:]), in_=per_slot(delta[:]), func=ACT.Copy, scale=cq[:])
-        nc.vector.scalar_tensor_tensor(out=spans(k[:]), in0=per_slot(gam[:]), scalar=cq[:], in1=spans(m[:]), op0=ALU.mult, op1=ALU.add)
-        nc.vector.tensor_tensor(out=f[:], in0=k[:], in1=w[:], op=ALU.mult)
-        nc.vector.tensor_tensor(out=window[:].indirect(offsets[:]), in0=f[:], in1=delta_slot[:], op=ALU.add)
+        def slots(x, h):
+            return x[:, h * HALF : (h + 1) * HALF]
 
-        for first, width, chunk in base_tiles:
-            nc.vector.tensor_tensor(out=chunk[:], in0=window[:, first : first + width], in1=chunk[:], op=ALU.add)
-            nc.sync.dma_start(out=out[:, first : first + width], in_=chunk[:])
+        def groups(x, h):
+            return x[:, h * HALF_G : (h + 1) * HALF_G]
+
+        def spread(x, h):
+            return per_slot(groups(x, h), HALF_G)
+
+        def stt(dst, in0, scalar, in1, op0, op1, accum=None):
+            nc.vector.scalar_tensor_tensor(out=dst, in0=in0, scalar=scalar, in1=in1, op0=op0, op1=op1, accum_out=accum)
+
+        def span_sum(dst, src, h):
+            nc.vector.tensor_reduce(out=groups(dst, h), in_=spans(src), axis=AX.X, op=ALU.add)
+
+        def make_t(h):
+            nc.scalar.activation(out=slots(t, h), in_=a_banks[h][:, 0:HALF], func=ACT.Tanh, scale=0.5)
+
+        def make_e(h):
+            stt(slots(e, h), slots(t, h), 1.0, u_banks[h][:, 0:HALF], ALU.add, ALU.mult)
+
+        def make_w(h):
+            stt(slots(w, h), slots(t, h), 1.0, slots(e, h), ALU.subtract, ALU.mult)
+            nc.scalar.activation(out=slots(w_sq, h), in_=slots(w, h), func=ACT.Square)
+
+        def make_tg(h):
+            stt(spans(slots(tg, h)), spans(slots(t, h)), cq[:], spread(r2, h), ALU.mult, ALU.mult)
+
+        def make_n0(h):
+            stt(spans(slots(n0, h)), spans(slots(w, h)), -4.0, spread(e_sum, h), ALU.mult, ALU.add)
+
+        make_t(0)
+        make_t(1)
+        cq = tile("cq", 1)
+        nc.scalar.activation(out=cq[:], in_=gq[:], func=ACT.Copy, scale=128.0)
+        make_e(0)
+        span_sum(s_sum, a_banks[0][:, 0:HALF], 0)
+        make_w(0)
+        span_sum(s_sum, a_banks[1][:, 0:HALF], 1)
+        make_e(1)
+        nc.vector.tensor_scalar(out=neg_s[:], in0=s_sum[:], scalar1=-1.0 / SPAN, scalar2=None, op0=ALU.mult, op1=ALU.min, accum_out=neg_max[:])
+        nc.scalar.activation(out=p[:], in_=neg_s[:], func=ACT.Exp, scale=-1.0, bias=neg_max[:], accum_out=z[:])
+        span_sum(e_sum, slots(e, 0), 0)
+        make_w(1)
+        nc.vector.reciprocal(out=rz[:], in_=z[:])
+        nc.scalar.activation(out=r[:], in_=p[:], func=ACT.Copy, scale=rz[:])
+        nc.scalar.activation(out=r2[:], in_=p[:], func=ACT.Square, scale=rz[:])
+        span_sum(e_sum, slots(e, 1), 1)
+        span_sum(w_sum, slots(w, 0), 0)
+        stt(re[:], e_sum, 1.0, r[:], ALU.mult, ALU.mult, d[:])
+        span_sum(w_sum, slots(w, 1), 1)
+        make_n0(0)
+        stt(g1[:], w_sum[:], -0.5, e_sum, ALU.mult, ALU.add)
+        nc.vector.tensor_tensor(out=g2, in0=e_sum, in1=w_sum[:], op=ALU.subtract)
+        span_sum(wsq_sum, slots(w_sq, 0), 0)
+        stt(rh[:], g1[:], d[:], r2[:], ALU.subtract, ALU.mult, hh[:])
+        stt(kr[:], ge[:], d[:], r[:].unsqueeze(1).to_broadcast([P, 2, G]), ALU.subtract, ALU.mult)
+        span_sum(wsq_sum, slots(w_sq, 1), 1)
+        stt(yr[:], kr[:, 0, :], hh[:], kr[:, 1, :], ALU.subtract, ALU.mult)
+        stt(gam[:], r[:], hh[:], rh[:], ALU.mult, ALU.subtract)
+        make_n0(1)
+        stt(zz[:], wsq_sum[:], -0.5, r2[:], ALU.mult, ALU.mult)
+        make_tg(0)
+        stt(qq[:], yr[:], -0.25, zz[:], ALU.mult, ALU.add, qbar[:])
+        make_tg(1)
+        stt(delta[:], r[:], qbar[:], qq[:], ALU.mult, ALU.subtract)
+        for h in range(2):
+            nc.scalar.activation(out=spans(slots(delta_slot, h)), in_=spread(delta, h), func=ACT.Copy, scale=cq[:])
+        for h in range(2):
+            stt(slots(m, h), slots(n0, h), d[:], slots(tg, h), ALU.subtract, ALU.mult)
+        for h in range(2):
+            stt(spans(slots(k, h)), spread(gam, h), cq[:], spans(slots(m, h)), ALU.mult, ALU.add)
+        for h in range(2):
+            nc.vector.tensor_tensor(out=slots(f, h), in0=slots(k, h), in1=slots(w, h), op=ALU.mult)
+        for h in range(2):
+            nc.vector.tensor_tensor(out=window[:].indirect(list_half(h)), in0=slots(f, h), in1=slots(delta_slot, h), op=ALU.add)
+
+        first = 0
+        for width in OUT_CHUNKS:
+            h, lo = divmod(first, T // 2)
+            chunk = base_halves[h][:, lo : lo + width]
+            nc.vector.tensor_tensor(out=chunk, in0=window[:, first : first + width], in1=chunk, op=ALU.add)
+            nc.sync.dma_start(out=out[:, first : first + width], in_=chunk)
+            first = first + width

@@ -47,29 +47,26 @@ def tile_attend_gpspanread_kernel(tc, query, keys_words, keys_scales, gout, vals
         v_words = tile("v_words", T, U16)
         k_words = tile("k_words", T, U16)
         gout_raw = sb.tile([P, PACK, Q], F32, name="gout_raw")
-        query_raw = sb.tile([P, PACK, Q], F32, name="query_raw")
+        query_raw = sb.tile([P, PACK, Q], F32, name="query_raw", tag="query_raw", align_bytes=64)
         size_col = tile("size_col", I // P)
         gq = tile("gq", 1)
         window = tile("window", T)
         ident = tile("ident", P)
-        warm = tile("warm", 1)
-        warm_out = tile("warm_out", 1)
 
-        nc.vector.memset(v_bytes[:].bitcast(I32), 0)
-        nc.gpsimd.memset(k_bytes[:].bitcast(I32), 0)
-        nc.vector.memset(warm[:], 0.0)
-        nc.scalar.activation(out=warm_out[:], in_=warm[:], func=ACT.Exp)
+        for plane in (v_bytes, k_bytes):
+            nc.vector.memset(plane[:, 0 : T // 2].bitcast(I32), 0)
+            nc.gpsimd.memset(plane[:, T // 2 : T].bitcast(I32), 0)
         nc.vector.memset(window[:].bitcast(I32), 0)
         make_identity(nc, ident[:])
 
         def load_scale_rows(dst, src):
-            for quad in range(4):
-                nc.sync.dma_start(out=dst[32 * quad : 32 * quad + 4, :].bitcast(I32), in_=src[0, 4 * quad : 4 * quad + 4, :].bitcast(I32))
+            for row in range(4):
+                nc.sync.dma_start(out=dst[row:P:32, :].bitcast(I32), in_=src[0, row:16:4, :].bitcast(I32))
 
         nc.sync.dma_start(offsets[:], offs)
         nc.sync.dma_start(out=v_words[:].bitcast(I32), in_=vals_words[0].bitcast(I32))
-        load_scale_rows(v_bytes, vals_scales)
         nc.sync.dma_start(out=gout_raw[:], in_=gout.rearrange("(p j) q -> p j q", j=PACK))
+        load_scale_rows(v_bytes, vals_scales)
         nc.sync.dma_start(out=k_words[:].bitcast(I32), in_=keys_words[0].bitcast(I32))
         with nc.allow_non_contiguous_dma(reason="one weight a slot, slots on the partitions"):
             nc.sync.dma_start(out=size_col[:], in_=size.rearrange("o (b p) -> p (o b)", p=P))
@@ -96,21 +93,21 @@ def tile_attend_gpspanread_kernel(tc, query, keys_words, keys_scales, gout, vals
         nc.vector.tensor_copy(vg_bytes[:], v_bytes[:].indirect(offsets[:]))
         gout_codes, gout_scales = quantize("gout", gout_bf)
 
-        c0_t = ps.tile([P, I], F32, name="c0_t")
-        u_t = tile("u_t", I)
+        c0_t = [ps.tile([P, I], F32, name="c0_t%d" % h, tag="product%d" % h) for h in range(2)]
+        u_t = sb.tile([P, I], F32, name="u_t", tag="query_raw", align_bytes=64)
         u_banks = [ps.tile([P, I], F32, name="u%d" % h) for h in range(2)]
         for b in range(I // P):
             cols = slice(b * P, (b + 1) * P)
-            nc.tensor.matmul_mx(out=c0_t[:, cols], lhsT=vg_words[:, cols].bitcast(FP4X4), lhsT_scale=vg_bytes[:, cols],
+            nc.tensor.matmul_mx(out=c0_t[b // 2][:, (b % 2) * P : (b % 2 + 1) * P], lhsT=vg_words[:, cols].bitcast(FP4X4), lhsT_scale=vg_bytes[:, cols],
                                 rhs=gout_codes[:].bitcast(FP8X4), rhs_scale=gout_scales[:], start=True, stop=True)
         for b in range(I // P):
             cols = slice(b * P, (b + 1) * P)
-            nc.scalar.activation(out=u_t[:, cols], in_=c0_t[:, cols], func=ACT.Copy, scale=size_col[:, b : b + 1])
+            nc.scalar.activation(out=u_t[:, cols], in_=c0_t[b // 2][:, (b % 2) * P : (b % 2 + 1) * P], func=ACT.Copy, scale=size_col[:, b : b + 1])
         for b in range(I // P):
             cols = slice(b * P, (b + 1) * P)
             nc.tensor.transpose(u_banks[b // 2][:, (b % 2) * P : (b % 2 + 1) * P], u_t[:, cols], ident[:])
 
-        a_banks = [ps.tile([P, I], F32, name="a%d" % h) for h in range(2)]
+        a_banks = [ps.tile([P, I], F32, name="a%d" % h, tag="product%d" % h) for h in range(2)]
 
         def list_half(h):
             return offsets[:, h * HALF // 16 : (h + 1) * HALF // 16]

from contextlib import ExitStack

import concourse.mybir as mybir
from concourse.masks import make_identity

D, T, I, Q, G = 512, 2048, 512, 128, 64
SPAN = I // G
P = 128
PACK = 4
HALF = I // 2
HALF_G = G // 2
FLOPS = 2 * 2 * Q * D * I

F32 = mybir.dt.float32
BF16 = mybir.dt.bfloat16
I32 = mybir.dt.int32
U32 = mybir.dt.uint32
U16 = mybir.dt.uint16
U8 = mybir.dt.uint8
FP8X4 = mybir.dt.float8_e4m3fn_x4
FP4X4 = mybir.dt.float4_e2m1fn_x4
ALU = mybir.AluOpType
ACT = mybir.ActivationFunctionType
AX = mybir.AxisListType

OUT_CHUNKS = (256, 384, 384, 384, 384, 256)


def tile_attend_gpspanread_kernel(tc, query, keys_words, keys_scales, gout, vals_words, vals_scales, size, base, gq1, offs, out):
    nc = tc.nc
    with ExitStack() as ctx:
        sb = ctx.enter_context(tc.tile_pool(name="sb", bufs=1))
        ps = ctx.enter_context(tc.psum_pool(name="ps", bufs=1))

        def tile(name, cols, dtype=F32):
            return sb.tile([P, cols], dtype, name=name, tag=name, align_bytes=64)

        def spans(ap):
            return ap.rearrange("p (g j) -> p g j", j=SPAN)

        def per_slot(ap, groups=G):
            return ap.unsqueeze(2).to_broadcast([P, groups, SPAN])

        offsets = sb.tile([P, I // 16], U16, name="offsets")
        v_bytes = tile("v_bytes", T, U8)
        k_bytes = tile("k_bytes", T, U8)
        v_words = tile("v_words", T, U16)
        k_words = tile("k_words", T, U16)
        gout_raw = sb.tile([P, PACK, Q], F32, name="gout_raw")
        query_raw = sb.tile([P, PACK, Q], F32, name="query_raw", tag="query_raw", align_bytes=64)
        size_col = tile("size_col", I // P)
        gq = tile("gq", 1)
        window = tile("window", T)
        ident = tile("ident", P)

        for plane in (v_bytes, k_bytes):
            nc.vector.memset(plane[:, 0 : T // 2].bitcast(I32), 0)
            nc.gpsimd.memset(plane[:, T // 2 : T].bitcast(I32), 0)
        nc.vector.memset(window[:].bitcast(I32), 0)
        make_identity(nc, ident[:])

        def load_scale_rows(dst, src):
            for row in range(4):
                nc.sync.dma_start(out=dst[row:P:32, :].bitcast(I32), in_=src[0, row:16:4, :].bitcast(I32))

        nc.sync.dma_start(offsets[:], offs)
        nc.sync.dma_start(out=v_words[:].bitcast(I32), in_=vals_words[0].bitcast(I32))
        nc.sync.dma_start(out=gout_raw[:], in_=gout.rearrange("(p j) q -> p j q", j=PACK))
        load_scale_rows(v_bytes, vals_scales)
        nc.sync.dma_start(out=k_words[:].bitcast(I32), in_=keys_words[0].bitcast(I32))
        with nc.allow_non_contiguous_dma(reason="one weight a slot, slots on the partitions"):
            nc.sync.dma_start(out=size_col[:], in_=size.rearrange("o (b p) -> p (o b)", p=P))
        nc.sync.dma_start(out=query_raw[:], in_=query.rearrange("(p j) q -> p j q", j=PACK))
        load_scale_rows(k_bytes, keys_scales)
        nc.sync.dma_start(out=gq[:], in_=gq1)

        def interleave(name, raw):
            grouped = sb.tile([P, Q, PACK], BF16, name=name, align_bytes=64)
            nc.scalar.copy(out=grouped[:], in_=raw[:].rearrange("p j q -> p q j"))
            return grouped

        def quantize(name, grouped):
            codes = tile(name + "_codes", Q, U32)
            scales = tile(name + "_scales", Q, U8)
            nc.vector.quantize_mx(out=codes[:].bitcast(FP8X4), scales=scales[:], in_=grouped[:].rearrange("p q j -> p (q j)"))
            return codes, scales

        gout_bf = interleave("gout_bf", gout_raw)
        query_bf = interleave("query_bf", query_raw)
        vg_bytes = tile("vg_bytes", I, U8)
        vg_words = tile("vg_words", I, U16)
        nc.vector.tensor_copy(vg_words[:], v_words[:].indirect(offsets[:]))
        nc.vector.tensor_copy(vg_bytes[:], v_bytes[:].indirect(offsets[:]))
        gout_codes, gout_scales = quantize("gout", gout_bf)

        c0_t = [ps.tile([P, I], F32, name="c0_t%d" % h, tag="product%d" % h) for h in range(2)]
        u_t = sb.tile([P, I], F32, name="u_t", tag="query_raw", align_bytes=64)
        u_banks = [ps.tile([P, I], F32, name="u%d" % h) for h in range(2)]
        for b in range(I // P):
            cols = slice(b * P, (b + 1) * P)
            nc.tensor.matmul_mx(out=c0_t[b // 2][:, (b % 2) * P : (b % 2 + 1) * P], lhsT=vg_words[:, cols].bitcast(FP4X4), lhsT_scale=vg_bytes[:, cols],
                                rhs=gout_codes[:].bitcast(FP8X4), rhs_scale=gout_scales[:], start=True, stop=True)
        for b in range(I // P):
            cols = slice(b * P, (b + 1) * P)
            nc.scalar.activation(out=u_t[:, cols], in_=c0_t[b // 2][:, (b % 2) * P : (b % 2 + 1) * P], func=ACT.Copy, scale=size_col[:, b : b + 1])
        for b in range(I // P):
            cols = slice(b * P, (b + 1) * P)
            nc.tensor.transpose(u_banks[b // 2][:, (b % 2) * P : (b % 2 + 1) * P], u_t[:, cols], ident[:])

        a_banks = [ps.tile([P, I], F32, name="a%d" % h, tag="product%d" % h) for h in range(2)]

        def list_half(h):
            return offsets[:, h * HALF // 16 : (h + 1) * HALF // 16]

        kg_words = tile("kg_words", I, U16)
        nc.vector.tensor_copy(kg_words[:], k_words[:].indirect(offsets[:]))
        query_codes, query_scales = quantize("query", query_bf)
        for h in range(2):
            kg_bytes = tile("kg_bytes%d" % h, HALF, U8)
            nc.vector.tensor_copy(kg_bytes[:], k_bytes[:].indirect(list_half(h)))
            nc.tensor.matmul_mx(out=a_banks[h][:, 0:HALF], lhsT=query_codes[:].bitcast(FP8X4), lhsT_scale=query_scales[:],
                                rhs=kg_words[:, h * HALF : (h + 1) * HALF].bitcast(FP4X4), rhs_scale=kg_bytes[:], start=True, stop=True)

        base_halves = []
        for h, tag in enumerate(("v_words", "k_words")):
            base_half = sb.tile([P, T // 2], F32, name="base%d" % h, tag=tag, align_bytes=64)
            nc.sync.dma_start(out=base_half[:], in_=base[:, h * T // 2 : (h + 1) * T // 2])
            base_halves.append(base_half)

        t = tile("t", I)
        e = tile("e", I)
        w = tile("w", I)
        w_sq = tile("w_sq", I)
        s_sum = tile("s_sum", G)
        neg_s = tile("neg_s", G)
        neg_max = tile("neg_max", 1)
        p = tile("p", G)
        z = tile("z", 1)
        rz = tile("rz", 1)
        r = tile("r", G)
        r2 = tile("r2", G)

        ge = sb.tile([P, 2, G], F32, name="ge")
        e_sum = ge[:, 1, :]
        g2 = ge[:, 0, :]
        w_sum = tile("w_sum", G)
        wsq_sum = tile("wsq_sum", G)
        re = tile("re", G)
        d = tile("d", 1)
        g1 = tile("g1", G)
        rh = tile("rh", G)
        hh = tile("hh", 1)
        kr = sb.tile([P, 2, G], F32, name="kr")
        gam = tile("gam", G)
        yr = tile("yr", G)
        zz = tile("zz", G)
        qq = tile("qq", G)
        qbar = tile("qbar", 1)
        delta = tile("delta", G)
        delta_slot = tile("delta_slot", I)
        tg = tile("tg", I)
        n0 = tile("n0", I)
        m = tile("m", I)
        k = tile("k", I)
        f = tile("f", I)

        def slots(x, h):
            return x[:, h * HALF : (h + 1) * HALF]

        def groups(x, h):
            return x[:, h * HALF_G : (h + 1) * HALF_G]

        def spread(x, h):
            return per_slot(groups(x, h), HALF_G)

        def stt(dst, in0, scalar, in1, op0, op1, accum=None):
            nc.vector.scalar_tensor_tensor(out=dst, in0=in0, scalar=scalar, in1=in1, op0=op0, op1=op1, accum_out=accum)

        def span_sum(dst, src, h):
            nc.vector.tensor_reduce(out=groups(dst, h), in_=spans(src), axis=AX.X, op=ALU.add)

        def make_t(h):
            nc.scalar.activation(out=slots(t, h), in_=a_banks[h][:, 0:HALF], func=ACT.Tanh, scale=0.5)

        def make_e(h):
            stt(slots(e, h), slots(t, h), 1.0, u_banks[h][:, 0:HALF], ALU.add, ALU.mult)

        def make_w(h):
            stt(slots(w, h), slots(t, h), 1.0, slots(e, h), ALU.subtract, ALU.mult)
            nc.scalar.activation(out=slots(w_sq, h), in_=slots(w, h), func=ACT.Square)

        def make_tg(h):
            stt(spans(slots(tg, h)), spans(slots(t, h)), cq[:], spread(r2, h), ALU.mult, ALU.mult)

        def make_n0(h):
            stt(spans(slots(n0, h)), spans(slots(w, h)), -4.0, spread(e_sum, h), ALU.mult, ALU.add)

        make_t(0)
        make_t(1)
        cq = tile("cq", 1)
        nc.scalar.activation(out=cq[:], in_=gq[:], func=ACT.Copy, scale=128.0)
        make_e(0)
        span_sum(s_sum, a_banks[0][:, 0:HALF], 0)
        make_w(0)
        span_sum(s_sum, a_banks[1][:, 0:HALF], 1)
        make_e(1)
        nc.vector.tensor_scalar(out=neg_s[:], in0=s_sum[:], scalar1=-1.0 / SPAN, scalar2=None, op0=ALU.mult, op1=ALU.min, accum_out=neg_max[:])
        nc.scalar.activation(out=p[:], in_=neg_s[:], func=ACT.Exp, scale=-1.0, bias=neg_max[:], accum_out=z[:])
        span_sum(e_sum, slots(e, 0), 0)
        make_w(1)
        nc.vector.reciprocal(out=rz[:], in_=z[:])
        nc.scalar.activation(out=r[:], in_=p[:], func=ACT.Copy, scale=rz[:])
        nc.scalar.activation(out=r2[:], in_=p[:], func=ACT.Square, scale=rz[:])
        span_sum(e_sum, slots(e, 1), 1)
        span_sum(w_sum, slots(w, 0), 0)
        stt(re[:], e_sum, 1.0, r[:], ALU.mult, ALU.mult, d[:])
        span_sum(w_sum, slots(w, 1), 1)
        make_n0(0)
        stt(g1[:], w_sum[:], -0.5, e_sum, ALU.mult, ALU.add)
        nc.vector.tensor_tensor(out=g2, in0=e_sum, in1=w_sum[:], op=ALU.subtract)
        span_sum(wsq_sum, slots(w_sq, 0), 0)
        stt(rh[:], g1[:], d[:], r2[:], ALU.subtract, ALU.mult, hh[:])
        stt(kr[:], ge[:], d[:], r[:].unsqueeze(1).to_broadcast([P, 2, G]), ALU.subtract, ALU.mult)
        span_sum(wsq_sum, slots(w_sq, 1), 1)
        stt(yr[:], kr[:, 0, :], hh[:], kr[:, 1, :], ALU.subtract, ALU.mult)
        stt(gam[:], r[:], hh[:], rh[:], ALU.mult, ALU.subtract)
        make_n0(1)
        stt(zz[:], wsq_sum[:], -0.5, r2[:], ALU.mult, ALU.mult)
        make_tg(0)
        stt(qq[:], yr[:], -0.25, zz[:], ALU.mult, ALU.add, qbar[:])
        make_tg(1)
        stt(delta[:], r[:], qbar[:], qq[:], ALU.mult, ALU.subtract)
        for h in range(2):
            nc.scalar.activation(out=spans(slots(delta_slot, h)), in_=spread(delta, h), func=ACT.Copy, scale=cq[:])
        for h in range(2):
            stt(slots(m, h), slots(n0, h), d[:], slots(tg, h), ALU.subtract, ALU.mult)
        for h in range(2):
            stt(spans(slots(k, h)), spread(gam, h), cq[:], spans(slots(m, h)), ALU.mult, ALU.add)
        for h in range(2):
            nc.vector.tensor_tensor(out=slots(f, h), in0=slots(k, h), in1=slots(w, h), op=ALU.mult)
        for h in range(2):
            nc.vector.tensor_tensor(out=window[:].indirect(list_half(h)), in0=slots(f, h), in1=slots(delta_slot, h), op=ALU.add)

        first = 0
        for width in OUT_CHUNKS:
            h, lo = divmod(first, T // 2)
            chunk = base_halves[h][:, lo : lo + width]
            nc.vector.tensor_tensor(out=chunk, in0=window[:, first : first + width], in1=chunk, op=ALU.add)
            nc.sync.dma_start(out=out[:, first : first + width], in_=chunk)
            first = first + width
